import numpy as np
import ml_dtypes


def mxq(x, axis, fmt="e4m3"):
    dtype, down = {"e4m3": (ml_dtypes.float8_e4m3fn, 7), "e5m2": (ml_dtypes.float8_e5m2, 14)}[fmt]
    v = np.moveaxis(np.asarray(x, np.float32).astype(ml_dtypes.bfloat16).astype(np.float64), axis, -1)
    blocks = v.reshape(v.shape[:-1] + (-1, 32))
    amax = np.abs(blocks).max(-1, keepdims=True)
    byte = np.maximum(np.where(amax > 0, np.frexp(amax)[1] - 1 + 127, 0) - down, 1)
    scale = np.exp2(byte - 127.0)
    codes = (blocks / scale).astype(np.float32).astype(dtype).astype(np.float64)
    return np.moveaxis((codes * scale).reshape(v.shape), -1, axis)


WIDE = False


def mx_kscale(k):
    if not WIDE:
        return np.ones(k)
    levels = np.array([10, -10, 5, -5, 0])
    if k % 512:
        return np.exp2(np.random.permutation(np.resize(levels, k // 32))).repeat(32)
    a = np.empty((k // 512, 16))
    for p in range(k // 512):
        a[p, :8] = np.random.permutation(np.resize(levels, 8))
        for g in range(8):
            far = levels[np.abs(levels - a[p, g]) >= 10]
            a[p, g + 8] = far[np.random.randint(len(far))]
    return np.exp2(a.ravel()).repeat(32)


def f64(x):
    return np.asarray(x).astype(np.float64)


def striped(idx):
    return np.tile(np.asarray(idx).reshape(-1, 16).T, (8, 1)).astype(np.uint16)


def unstriped(offs):
    return offs[:16].T.reshape(-1).astype(np.int64)


E2M1 = np.array([0.0, 0.5, 1.0, 1.5, 2.0, 3.0, 4.0, 6.0, -0.0, -0.5, -1.0, -1.5, -2.0, -3.0, -4.0, -6.0])


def pack_weight(w, fmt):
    k, n = w.shape
    w = f64(np.asarray(w, np.float32).astype(ml_dtypes.bfloat16)).reshape(k // 32, 32, n)
    amax = np.abs(w).max(1)
    if fmt == "e4m3":
        byte = np.frexp(amax)[1] - 1 + 127 - 7
    else:
        mant, ex = np.frexp(amax / 6.0)
        byte = np.where(mant > 0.5, ex, ex - 1) + 127
    byte = np.clip(np.where(amax > 0, byte, 1), 1, 254)
    scaled = (w * np.exp2(127.0 - byte)[:, None, :]).reshape(k, n).astype(np.float32)
    by_word = np.ascontiguousarray(scaled.reshape(k // 512, 128, 4, n).transpose(0, 1, 3, 2))
    if fmt == "e4m3":
        words = by_word.astype(ml_dtypes.float8_e4m3fn).view(np.uint8)
    else:
        c = by_word.astype(ml_dtypes.float4_e2m1fn).view(np.uint8) & 0xF
        words = (c[..., 0::2] | (c[..., 1::2] << 4)).reshape(k // 512, 128, 2 * n)
    return np.ascontiguousarray(words), np.ascontiguousarray(byte.astype(np.uint8).reshape(k // 512, 16, n))


def unpack_weight(words, scales, fmt):
    g, _, n = scales.shape
    words = np.ascontiguousarray(words).reshape(g, 128, n, -1)
    if fmt == "e4m3":
        vals = words.view(ml_dtypes.float8_e4m3fn).astype(np.float64)
    else:
        nib = np.empty((g, 128, n, 4), np.uint8)
        nib[..., 0::2] = words & 0xF
        nib[..., 1::2] = words >> 4
        vals = E2M1[nib]
    vals = vals * np.repeat(np.exp2(scales.astype(np.float64) - 127.0), 8, axis=1)[..., None]
    return vals.transpose(0, 1, 3, 2).reshape(g * 512, n)


def sigmoid(v):
    return 1.0 / (1.0 + np.exp(-v))


D, K, R, T, I, Q, G, U = 512, 512, 512, 2048, 512, 128, 64, 1024


def setup_inputs():
    n = np.random.standard_normal
    idx2 = np.random.permutation(U)[:I]
    idx = np.random.permutation(T)[:I]
    fd = mx_kscale(D)
    fk = mx_kscale(K)
    fr = mx_kscale(R)
    keysp = pack_weight(n((D, T)) / fd[:, None], "e2m1")
    tabp = pack_weight(n((K, T)) / fk[:, None], "e2m1")
    return {
        "query": (n((D, Q)) * 0.6 / np.sqrt(D) * fd[:, None]).astype(np.float32),
        "keys_words": keysp[0],
        "keys_scales": keysp[1],
        "sharp": (np.random.uniform(1.0, 3.0, (Q, 1))).astype(np.float32),
        "tab_words": tabp[0],
        "tab_scales": tabp[1],
        "w1": (n((K, R)) * 1 / np.sqrt(K) * fk[:, None]).astype(np.float32),
        "gtab": (n((R, U))).astype(np.float32),
        "gout": (n((R, Q)) * 1 / np.sqrt(R) * fr[:, None]).astype(np.float32),
        "hsc": (np.random.uniform(0.7, 1.4, (R, 1)) / fr[:, None]).astype(np.float32),
        "old": (0.5 * n((Q, T))).astype(np.float32),
        "offs2": striped(idx2),
        "offs": striped(idx),
    }


def reference(query, keys_words, keys_scales, sharp, tab_words, tab_scales, w1, gtab, gout, hsc, old, offs2, offs):
    idx2 = unstriped(offs2)
    idx = unstriped(offs)
    keysu = unpack_weight(keys_words, keys_scales, "e2m1")
    tabu = unpack_weight(tab_words, tab_scales, "e2m1")
    queryq = mxq(f64(query), 0, "e4m3")
    keysidxg = keysu[:, idx]
    a = queryq.T @ keysidxg
    p = np.exp(a)
    s = p.reshape(Q, G, I // G).sum(axis=2)
    ms = a.reshape(Q, G, I // G).mean(axis=2) * f64(sharp)
    pg = np.exp(ms - np.max(ms, axis=1, keepdims=True))
    z = np.sum(pg, axis=1, keepdims=True)
    sh = pg / z / s
    rr = np.repeat(sh, I // G, axis=1)
    w1q = mxq(f64(w1), 0, "e4m3")
    tabidxg = tabu[:, idx]
    zh = w1q.T @ tabidxg
    hg = sigmoid(f64(gtab)[:, idx2])
    hv = zh * hg
    hs1 = hv * f64(hsc)
    goutq = mxq(f64(gout), 0, "e4m3")
    hs1q = mxq(hs1, 0, "e4m3")
    c0 = goutq.T @ hs1q
    drr = c0 * p
    dsh = drr.reshape(Q, G, I // G).sum(axis=2)
    dz = np.sum(dsh / s * pg / np.square(z) * (-1.0), axis=1, keepdims=True)
    dpg = dsh / s / z + dz
    dms = dpg * pg
    e1 = dms * f64(sharp) / 8.0
    r1 = np.repeat(e1, I // G, axis=1)
    ds = dsh * pg / z / np.square(s) * (-1.0)
    r2 = np.repeat(ds, I // G, axis=1)
    dp = c0 * rr + r2
    da = r1 + dp * p
    gs = da * 512.0
    gf = np.zeros((Q, T))
    gf[:, idx] = gs
    y = f64(old) + gf
    return y

@@ -1,0 +1,204 @@
+from contextlib import ExitStack
+
+import concourse.mybir as mybir
+
+D, K, R, T, I, Q, G, U = 512, 512, 512, 2048, 512, 128, 64, 1024
+FLOPS = 2 * D * Q * I + 2 * K * R * I + 2 * R * Q * I
+
+F32 = mybir.dt.float32
+BF16 = mybir.dt.bfloat16
+I32 = mybir.dt.int32
+U32 = mybir.dt.uint32
+U16 = mybir.dt.uint16
+U8 = mybir.dt.uint8
+FP8X4 = mybir.dt.float8_e4m3fn_x4
+FP4X4 = mybir.dt.float4_e2m1fn_x4
+ALU = mybir.AluOpType
+ACT = mybir.ActivationFunctionType
+AX = mybir.AxisListType
+
+P = 128
+PACK = 4
+GROUP = I // G
+STORE_COLS = [256, 512, 512, 512, 256]
+HALF = I // 2
+HS_SPLIT = 352
+
+
+def tile_attend_blrgated_bygroup_kernel(tc, query, keys_words, keys_scales, sharp, tab_words, tab_scales,
+                                         w1, gtab, gout, hsc, old, offs2, offs, out):
+    nc = tc.nc
+    with ExitStack() as ctx:
+        lists = ctx.enter_context(tc.tile_pool(name="lists", bufs=1))
+        sb = ctx.enter_context(tc.tile_pool(name="sb", bufs=1))
+        ps = ctx.enter_context(tc.psum_pool(name="ps", bufs=1))
+
+        def tile(name, shape, dtype, tag=None):
+            return sb.tile(shape, dtype, name=name, tag=tag or name, align_bytes=64)
+
+        def by_group(ap):
+            return ap.rearrange("p (g j) -> p g j", j=GROUP)
+
+        def spread(ap):
+            return ap.unsqueeze(2).to_broadcast([P, ap.shape[1], GROUP])
+
+        def load_scale_rows(engine, plane, scales):
+            for quad in range(4):
+                engine.dma_start(out=plane[32 * quad:32 * quad + 4, :].bitcast(I32),
+                                 in_=scales[0, 4 * quad:4 * quad + 4, :].bitcast(I32))
+
+        slots = lists.tile([P, I // 16], U16, name="slots")
+        gates = lists.tile([P, I // 16], U16, name="gates")
+        key_bytes = tile("key_bytes", [P, T], U8)
+        tab_bytes = tile("tab_bytes", [P, T], U8)
+        scattered = tile("scattered", [P, T], F32)
+        nc.gpsimd.memset(key_bytes[:].bitcast(I32), 0)
+        nc.gpsimd.memset(tab_bytes[:].bitcast(I32), 0)
+        nc.gpsimd.memset(scattered[:], 0.0)
+
+        q_raw = tile("q_raw", [P, PACK, Q], F32)
+        key_pool = tile("key_pool", [P, T], U16)
+        tab_pool = tile("tab_pool", [P, T], U16)
+        w_raw = [tile("w_raw%d" % h, [P, PACK, R // 2], F32) for h in range(2)]
+        g_raw = tile("g_raw", [P, PACK, Q], F32)
+        gate_pool = [tile("gate_pool%d" % t, [P, U], F32) for t in range(PACK)]
+        old_sb = tile("old_sb", [P, T], F32)
+        sharp_sb = tile("sharp_sb", [P, 1], F32)
+        hsc_sb = tile("hsc_sb", [P, PACK], F32)
+        gtab_planes = gtab.rearrange("(p t) u -> t p u", t=PACK)
+        w_rows = w1.rearrange("(p j) c -> p j c", j=PACK)
+
+        nc.sync.dma_start(slots[:], offs)
+        nc.sync.dma_start(out=key_pool[:].bitcast(I32), in_=keys_words[0].bitcast(I32))
+        load_scale_rows(nc.sync, key_bytes, keys_scales)
+        nc.sync.dma_start(out=q_raw[:], in_=query.rearrange("(p j) c -> p j c", j=PACK))
+        nc.scalar.dma_start(out=sharp_sb[:], in_=sharp)
+        nc.sync.dma_start(out=w_raw[0][:], in_=w_rows[:, :, 0:R // 2])
+        nc.sync.dma_start(out=tab_pool[:].bitcast(I32), in_=tab_words[0].bitcast(I32))
+        load_scale_rows(nc.sync, tab_bytes, tab_scales)
+        nc.sync.dma_start(out=w_raw[1][:], in_=w_rows[:, :, R // 2:R])
+        nc.sync.dma_start(gates[:], offs2)
+        nc.sync.dma_start(out=gate_pool[0][:], in_=gtab_planes[0])
+        nc.sync.dma_start(out=gate_pool[1][:], in_=gtab_planes[1])
+        nc.sync.dma_start(out=hsc_sb[:], in_=hsc.rearrange("(p t) o -> p (t o)", t=PACK))
+        nc.sync.dma_start(out=gate_pool[2][:], in_=gtab_planes[2])
+        nc.sync.dma_start(out=gate_pool[3][:], in_=gtab_planes[3])
+        nc.sync.dma_start(out=g_raw[:], in_=gout.rearrange("(p j) c -> p j c", j=PACK))
+        nc.sync.dma_start(out=old_sb[:], in_=old)
+
+        def interleaved_views(dst, src):
+            return (dst.rearrange("p (c i j) -> p c j i", i=4, j=PACK), src.rearrange("p j (c i) -> p c j i", i=4))
+
+        def quantise(name, values, width):
+            codes = tile(name + "_codes", [P, width], U32)
+            plane = tile(name + "_plane", [P, width], U8)
+            nc.vector.quantize_mx(out=codes[:].bitcast(FP8X4), scales=plane[:], in_=values)
+            return codes, plane
+
+        halves = [slice(h * HALF, (h + 1) * HALF) for h in range(2)]
+        group_halves = [slice(h * G // 2, (h + 1) * G // 2) for h in range(2)]
+
+        key_scale = tile("key_scale", [P, I], U8)
+        key_codes = tile("key_codes", [P, I], U16)
+        q_bf = tile("q_bf", [P, PACK * Q], BF16)
+        neg_k = tile("neg_k", [P, 1], F32)
+        nc.scalar.activation(neg_k[:], sharp_sb[:], ACT.Copy, scale=-1.0 / GROUP)
+        nc.vector.tensor_copy(key_codes[:], key_pool[:].indirect(slots[:]))
+        nc.vector.tensor_copy(key_scale[:], key_bytes[:].indirect(slots[:]))
+        dst, src = interleaved_views(q_bf[:], q_raw[:])
+        nc.scalar.copy(out=dst, in_=src)
+        q_codes, q_plane = quantise("q", q_bf[:], Q)
+        score_sum = tile("score_sum", [P, G], F32)
+        p = tile("p", [P, I], F32)
+        scores = [ps.tile([P, HALF], F32, name="score%d" % h, tag="half%d" % h) for h in range(2)]
+        for h in range(2):
+            nc.tensor.matmul_mx(out=scores[h][:], lhsT=q_codes[:].bitcast(FP8X4), lhsT_scale=q_plane[:],
+                                rhs=key_codes[:, halves[h]].bitcast(FP4X4), rhs_scale=key_scale[:, halves[h]],
+                                start=True, stop=True)
+        for h in range(2):
+            nc.vector.tensor_reduce(score_sum[:, group_halves[h]], by_group(scores[h][:]), AX.X, ALU.add)
+            nc.scalar.activation(p[:, halves[h]], scores[h][:], ACT.Exp)
+        neg_ms = tile("neg_ms", [P, G], F32)
+        neg_top = tile("neg_top", [P, 1], F32, tag="gate")
+        nc.vector.tensor_scalar(neg_ms[:], score_sum[:], neg_k[:], None, ALU.mult, ALU.min, accum_out=neg_top[:])
+        pg = tile("pg", [P, G], F32)
+        sums = tile("sums", [P, G + 1], F32)
+        nc.scalar.activation(pg[:], neg_ms[:], ACT.Exp, bias=neg_top[:], scale=-1.0, accum_out=sums[:, G:G + 1])
+
+        tab_codes = tile("tab_codes", [P, I], U16, tag="score_sum")
+        tab_scale = tile("tab_scale", [P, I], U8, tag="neg_ms")
+        nc.vector.tensor_copy(tab_codes[:], tab_pool[:].indirect(slots[:]))
+        nc.vector.tensor_copy(tab_scale[:], tab_bytes[:].indirect(slots[:]))
+
+        w_bf = tile("w_bf", [P, PACK * R], BF16)
+        w_dealt = w_bf[:].rearrange("p (t m j) -> p m j t", t=PACK, j=PACK)
+        nc.scalar.copy(out=w_dealt[:, 0:P // 2], in_=w_raw[0][:].rearrange("p j (m t) -> p m j t", t=PACK))
+        nc.vector.tensor_copy(out=w_dealt[:, P // 2:P], in_=w_raw[1][:].rearrange("p j (m t) -> p m j t", t=PACK))
+        w_codes, w_plane = quantise("w", w_bf[:], R)
+
+        zh = [ps.tile([P, I], F32, name="zh%d" % t) for t in range(PACK)]
+        for t in range(PACK):
+            rows = slice(t * P, (t + 1) * P)
+            nc.tensor.matmul_mx(out=zh[t][:], lhsT=w_codes[:, rows].bitcast(FP8X4), lhsT_scale=w_plane[:, rows],
+                                rhs=tab_codes[:].bitcast(FP4X4), rhs_scale=tab_scale[:], start=True, stop=True)
+
+        nc.vector.tensor_reduce(sums[:, 0:G], by_group(p[:]), AX.X, ALU.add)
+        inv = tile("inv", [P, G + 1], F32, tag="w_bf")
+        nc.vector.reciprocal(inv[:], sums[:])
+        neg_share = tile("neg_share", [P, I], F32)
+        nc.vector.scalar_tensor_tensor(by_group(neg_share[:]), by_group(p[:]), -1.0, spread(inv[:, 0:G]),
+                                       ALU.mult, ALU.mult)
+        neg_pi512 = tile("neg_pi512", [P, G], F32)
+        neg_pik = tile("neg_pik", [P, G], F32)
+        nc.vector.tensor_scalar(neg_pi512[:], pg[:], inv[:, G:G + 1], -512.0, ALU.mult, ALU.mult)
+        nc.vector.tensor_scalar(neg_pik[:], pg[:], inv[:, G:G + 1], neg_k[:], ALU.mult, ALU.mult)
+        weight = tile("weight", [P, I], F32)
+        nc.vector.tensor_tensor(by_group(weight[:]), by_group(neg_share[:]), spread(neg_pi512[:]), ALU.mult)
+
+        gate = tile("gate", [P, PACK, I], F32)
+        hs_planes = tile("hs_planes", [P, PACK, I], BF16)
+        for t in range(PACK):
+            nc.scalar.activation(gate[:, t, :], gate_pool[t][:].indirect(gates[:]), ACT.Sigmoid)
+            nc.vector.scalar_tensor_tensor(hs_planes[:, t, :], zh[t][:], hsc_sb[:, t:t + 1], gate[:, t, :],
+                                           ALU.mult, ALU.mult)
+        g_bf = tile("g_bf", [P, PACK * Q], BF16)
+        dst, src = interleaved_views(g_bf[:], g_raw[:])
+        nc.scalar.copy(out=dst, in_=src)
+        g_codes, g_plane = quantise("g", g_bf[:], Q)
+
+        hs_bf = tile("hs_bf", [P, PACK * I], BF16)
+        dst, src = interleaved_views(hs_bf[:, 0:PACK * HS_SPLIT], hs_planes[:, :, 0:HS_SPLIT])
+        nc.vector.tensor_copy(out=dst, in_=src)
+        dst, src = interleaved_views(hs_bf[:, PACK * HS_SPLIT:], hs_planes[:, :, HS_SPLIT:])
+        nc.scalar.copy(out=dst, in_=src)
+
+        wc = tile("wc", [P, I], F32)
+        half_total = tile("half_total", [P, 2], F32)
+        c0 = []
+        for h in range(2):
+            hs_codes, hs_plane = quantise("hs%d" % h, hs_bf[:, PACK * h * HALF:PACK * (h + 1) * HALF], HALF)
+            c0.append(ps.tile([P, HALF], F32, name="c0_%d" % h, tag="half%d" % h))
+            nc.tensor.matmul_mx(out=c0[h][:], lhsT=g_codes[:].bitcast(FP8X4), lhsT_scale=g_plane[:],
+                                rhs=hs_codes[:].bitcast(FP8X4), rhs_scale=hs_plane[:], start=True, stop=True)
+        for h in range(2):
+            nc.vector.scalar_tensor_tensor(wc[:, halves[h]], c0[h][:], 1.0, weight[:, halves[h]], ALU.mult, ALU.mult,
+                                           accum_out=half_total[:, h:h + 1])
+        row_total = tile("row_total", [P, 1], F32)
+        nc.scalar.activation(row_total[:], half_total[:, 1:2], ACT.Identity, bias=half_total[:, 0:1])
+        group_total = tile("group_total", [P, G], F32)
+        nc.vector.tensor_reduce(group_total[:], by_group(wc[:]), AX.X, ALU.add)
+        own = tile("own", [P, I], F32)
+        nc.vector.scalar_tensor_tensor(by_group(own[:]), spread(neg_pik[:]), row_total[:], by_group(wc[:]),
+                                       ALU.mult, ALU.add)
+        shared = tile("shared", [P, I], F32)
+        nc.vector.scalar_tensor_tensor(by_group(shared[:]), by_group(neg_share[:]), neg_k[:], spread(group_total[:]),
+                                       ALU.subtract, ALU.mult)
+        nc.vector.tensor_tensor(scattered[:].indirect(slots[:]), own[:], shared[:], ALU.add)
+
+        first = 0
+        for n, width in enumerate(STORE_COLS):
+            cols = slice(first, first + width)
+            result = tile("result%d" % n, [P, width], F32)
+            nc.vector.tensor_tensor(result[:], scattered[:, cols], old_sb[:, cols], ALU.add)
+            nc.sync.dma_start(out=out[:, cols], in_=result[:])
+            first += width

@@ -22,7 +22,7 @@ PACK = 4
 GROUP = I // G
 STORE_COLS = [256, 512, 512, 512, 256]
 HALF = I // 2
-HS_SPLIT = 352
+HS_SPLIT = 320
 
 
 def tile_attend_blrgated_bygroup_kernel(tc, query, keys_words, keys_scales, sharp, tab_words, tab_scales,
@@ -52,9 +52,9 @@ def tile_attend_blrgated_bygroup_kernel(tc, query, keys_words, keys_scales, shar
         key_bytes = tile("key_bytes", [P, T], U8)
         tab_bytes = tile("tab_bytes", [P, T], U8)
         scattered = tile("scattered", [P, T], F32)
-        nc.gpsimd.memset(key_bytes[:].bitcast(I32), 0)
-        nc.gpsimd.memset(tab_bytes[:].bitcast(I32), 0)
-        nc.gpsimd.memset(scattered[:], 0.0)
+        nc.vector.memset(key_bytes[:].bitcast(I32), 0)
+        nc.vector.memset(tab_bytes[:].bitcast(I32), 0)
+        nc.vector.memset(scattered[:], 0.0)
 
         q_raw = tile("q_raw", [P, PACK, Q], F32)
         key_pool = tile("key_pool", [P, T], U16)
@@ -73,12 +73,12 @@ def tile_attend_blrgated_bygroup_kernel(tc, query, keys_words, keys_scales, shar
         load_scale_rows(nc.sync, key_bytes, keys_scales)
         nc.sync.dma_start(out=q_raw[:], in_=query.rearrange("(p j) c -> p j c", j=PACK))
         nc.scalar.dma_start(out=sharp_sb[:], in_=sharp)
-        nc.sync.dma_start(out=w_raw[0][:], in_=w_rows[:, :, 0:R // 2])
-        nc.sync.dma_start(out=tab_pool[:].bitcast(I32), in_=tab_words[0].bitcast(I32))
+        for h in range(2):
+            nc.sync.dma_start(out=w_raw[h][:], in_=w_rows[:, :, h * (R // 2):(h + 1) * (R // 2)])
         load_scale_rows(nc.sync, tab_bytes, tab_scales)
-        nc.sync.dma_start(out=w_raw[1][:], in_=w_rows[:, :, R // 2:R])
         nc.sync.dma_start(gates[:], offs2)
         nc.sync.dma_start(out=gate_pool[0][:], in_=gtab_planes[0])
+        nc.sync.dma_start(out=tab_pool[:].bitcast(I32), in_=tab_words[0].bitcast(I32))
         nc.sync.dma_start(out=gate_pool[1][:], in_=gtab_planes[1])
         nc.sync.dma_start(out=hsc_sb[:], in_=hsc.rearrange("(p t) o -> p (t o)", t=PACK))
         nc.sync.dma_start(out=gate_pool[2][:], in_=gtab_planes[2])
@@ -89,8 +89,8 @@ def tile_attend_blrgated_bygroup_kernel(tc, query, keys_words, keys_scales, shar
         def interleaved_views(dst, src):
             return (dst.rearrange("p (c i j) -> p c j i", i=4, j=PACK), src.rearrange("p j (c i) -> p c j i", i=4))
 
-        def quantise(name, values, width):
-            codes = tile(name + "_codes", [P, width], U32)
+        def quantise(name, values, width, tag=None):
+            codes = tile(name + "_codes", [P, width], U32, tag)
             plane = tile(name + "_plane", [P, width], U8)
             nc.vector.quantize_mx(out=codes[:].bitcast(FP8X4), scales=plane[:], in_=values)
             return codes, plane
@@ -108,9 +108,13 @@ def tile_attend_blrgated_bygroup_kernel(tc, query, keys_words, keys_scales, shar
         dst, src = interleaved_views(q_bf[:], q_raw[:])
         nc.scalar.copy(out=dst, in_=src)
         q_codes, q_plane = quantise("q", q_bf[:], Q)
-        score_sum = tile("score_sum", [P, G], F32)
-        p = tile("p", [P, I], F32)
-        scores = [ps.tile([P, HALF], F32, name="score%d" % h, tag="half%d" % h) for h in range(2)]
+        w_bf = tile("w_bf", [P, PACK * R], BF16)
+        w_dealt = w_bf[:].rearrange("p (t m j) -> p m j t", t=PACK, j=PACK)
+        nc.scalar.copy(out=w_dealt[:, 0:P // 2], in_=w_raw[0][:].rearrange("p j (m t) -> p m j t", t=PACK))
+        nc.vector.tensor_copy(out=w_dealt[:, P // 2:P], in_=w_raw[1][:].rearrange("p j (m t) -> p m j t", t=PACK))
+        score_sum = tile("score_sum", [P, G], F32, tag="w_raw1")
+        p = tile("p", [P, I], F32, tag="w_raw0")
+        scores = [ps.tile([P, HALF], F32, name="score%d" % h) for h in range(2)]
         for h in range(2):
             nc.tensor.matmul_mx(out=scores[h][:], lhsT=q_codes[:].bitcast(FP8X4), lhsT_scale=q_plane[:],
                                 rhs=key_codes[:, halves[h]].bitcast(FP4X4), rhs_scale=key_scale[:, halves[h]],
@@ -122,19 +126,14 @@ def tile_attend_blrgated_bygroup_kernel(tc, query, keys_words, keys_scales, shar
         neg_top = tile("neg_top", [P, 1], F32, tag="gate")
         nc.vector.tensor_scalar(neg_ms[:], score_sum[:], neg_k[:], None, ALU.mult, ALU.min, accum_out=neg_top[:])
         pg = tile("pg", [P, G], F32)
-        sums = tile("sums", [P, G + 1], F32)
-        nc.scalar.activation(pg[:], neg_ms[:], ACT.Exp, bias=neg_top[:], scale=-1.0, accum_out=sums[:, G:G + 1])
+        pg_sum = tile("pg_sum", [P, 1], F32)
+        nc.scalar.activation(pg[:], neg_ms[:], ACT.Exp, bias=neg_top[:], scale=-1.0, accum_out=pg_sum[:])
 
-        tab_codes = tile("tab_codes", [P, I], U16, tag="score_sum")
+        w_codes, w_plane = quantise("w", w_bf[:], R, tag="w_raw1")
         tab_scale = tile("tab_scale", [P, I], U8, tag="neg_ms")
-        nc.vector.tensor_copy(tab_codes[:], tab_pool[:].indirect(slots[:]))
+        tab_codes = tile("tab_codes", [P, I], U16)
         nc.vector.tensor_copy(tab_scale[:], tab_bytes[:].indirect(slots[:]))
-
-        w_bf = tile("w_bf", [P, PACK * R], BF16)
-        w_dealt = w_bf[:].rearrange("p (t m j) -> p m j t", t=PACK, j=PACK)
-        nc.scalar.copy(out=w_dealt[:, 0:P // 2], in_=w_raw[0][:].rearrange("p j (m t) -> p m j t", t=PACK))
-        nc.vector.tensor_copy(out=w_dealt[:, P // 2:P], in_=w_raw[1][:].rearrange("p j (m t) -> p m j t", t=PACK))
-        w_codes, w_plane = quantise("w", w_bf[:], R)
+        nc.vector.tensor_copy(tab_codes[:], tab_pool[:].indirect(slots[:]))
 
         zh = [ps.tile([P, I], F32, name="zh%d" % t) for t in range(PACK)]
         for t in range(PACK):
@@ -142,18 +141,12 @@ def tile_attend_blrgated_bygroup_kernel(tc, query, keys_words, keys_scales, shar
             nc.tensor.matmul_mx(out=zh[t][:], lhsT=w_codes[:, rows].bitcast(FP8X4), lhsT_scale=w_plane[:, rows],
                                 rhs=tab_codes[:].bitcast(FP4X4), rhs_scale=tab_scale[:], start=True, stop=True)
 
-        nc.vector.tensor_reduce(sums[:, 0:G], by_group(p[:]), AX.X, ALU.add)
-        inv = tile("inv", [P, G + 1], F32, tag="w_bf")
-        nc.vector.reciprocal(inv[:], sums[:])
-        neg_share = tile("neg_share", [P, I], F32)
-        nc.vector.scalar_tensor_tensor(by_group(neg_share[:]), by_group(p[:]), -1.0, spread(inv[:, 0:G]),
-                                       ALU.mult, ALU.mult)
-        neg_pi512 = tile("neg_pi512", [P, G], F32)
-        neg_pik = tile("neg_pik", [P, G], F32)
-        nc.vector.tensor_scalar(neg_pi512[:], pg[:], inv[:, G:G + 1], -512.0, ALU.mult, ALU.mult)
-        nc.vector.tensor_scalar(neg_pik[:], pg[:], inv[:, G:G + 1], neg_k[:], ALU.mult, ALU.mult)
-        weight = tile("weight", [P, I], F32)
-        nc.vector.tensor_tensor(by_group(weight[:]), by_group(neg_share[:]), spread(neg_pi512[:]), ALU.mult)
+        p_sum = tile("p_sum", [P, G], F32, tag="tab_pool")
+        inv_s = tile("inv_s", [P, G], F32)
+        inv_z = tile("inv_z", [P, 1], F32, tag="tab_bytes")
+        nc.vector.tensor_reduce(p_sum[:], by_group(p[:]), AX.X, ALU.add)
+        nc.vector.reciprocal(inv_z[:], pg_sum[:])
+        nc.vector.reciprocal(inv_s[:], p_sum[:])
 
         gate = tile("gate", [P, PACK, I], F32)
         hs_planes = tile("hs_planes", [P, PACK, I], BF16)
@@ -161,6 +154,7 @@ def tile_attend_blrgated_bygroup_kernel(tc, query, keys_words, keys_scales, shar
             nc.scalar.activation(gate[:, t, :], gate_pool[t][:].indirect(gates[:]), ACT.Sigmoid)
             nc.vector.scalar_tensor_tensor(hs_planes[:, t, :], zh[t][:], hsc_sb[:, t:t + 1], gate[:, t, :],
                                            ALU.mult, ALU.mult)
+
         g_bf = tile("g_bf", [P, PACK * Q], BF16)
         dst, src = interleaved_views(g_bf[:], g_raw[:])
         nc.scalar.copy(out=dst, in_=src)
@@ -172,23 +166,35 @@ def tile_attend_blrgated_bygroup_kernel(tc, query, keys_words, keys_scales, shar
         dst, src = interleaved_views(hs_bf[:, PACK * HS_SPLIT:], hs_planes[:, :, HS_SPLIT:])
         nc.scalar.copy(out=dst, in_=src)
 
+        neg_share = tile("neg_share", [P, I], F32, tag="gate_pool2")
+        nc.vector.scalar_tensor_tensor(by_group(neg_share[:]), by_group(p[:]), -1.0, spread(inv_s[:]),
+                                       ALU.mult, ALU.mult)
+        weight = tile("weight", [P, I], F32)
+        nc.vector.scalar_tensor_tensor(by_group(weight[:]), by_group(neg_share[:]), inv_z[:], spread(pg[:]),
+                                       ALU.mult, ALU.mult)
+
         wc = tile("wc", [P, I], F32)
         half_total = tile("half_total", [P, 2], F32)
         c0 = []
         for h in range(2):
             hs_codes, hs_plane = quantise("hs%d" % h, hs_bf[:, PACK * h * HALF:PACK * (h + 1) * HALF], HALF)
-            c0.append(ps.tile([P, HALF], F32, name="c0_%d" % h, tag="half%d" % h))
+            c0.append(ps.tile([P, HALF], F32, name="c0_%d" % h))
             nc.tensor.matmul_mx(out=c0[h][:], lhsT=g_codes[:].bitcast(FP8X4), lhsT_scale=g_plane[:],
                                 rhs=hs_codes[:].bitcast(FP8X4), rhs_scale=hs_plane[:], start=True, stop=True)
         for h in range(2):
-            nc.vector.scalar_tensor_tensor(wc[:, halves[h]], c0[h][:], 1.0, weight[:, halves[h]], ALU.mult, ALU.mult,
+            nc.vector.scalar_tensor_tensor(wc[:, halves[h]], c0[h][:], -512.0, weight[:, halves[h]], ALU.mult, ALU.mult,
                                            accum_out=half_total[:, h:h + 1])
+        row_factor = tile("row_factor", [P, 1], F32, tag="gate_pool3")
+        first_term = tile("first_term", [P, 1], F32)
         row_total = tile("row_total", [P, 1], F32)
-        nc.scalar.activation(row_total[:], half_total[:, 1:2], ACT.Identity, bias=half_total[:, 0:1])
+        nc.scalar.activation(row_factor[:], inv_z[:], ACT.Copy, scale=neg_k[:])
+        nc.scalar.activation(first_term[:], half_total[:, 0:1], ACT.Copy, scale=row_factor[:])
+        nc.scalar.activation(row_total[:], half_total[:, 1:2], ACT.Identity, bias=first_term[:], scale=row_factor[:])
         group_total = tile("group_total", [P, G], F32)
-        nc.vector.tensor_reduce(group_total[:], by_group(wc[:]), AX.X, ALU.add)
+        for h in range(2):
+            nc.vector.tensor_reduce(group_total[:, group_halves[h]], by_group(wc[:, halves[h]]), AX.X, ALU.add)
         own = tile("own", [P, I], F32)
-        nc.vector.scalar_tensor_tensor(by_group(own[:]), spread(neg_pik[:]), row_total[:], by_group(wc[:]),
+        nc.vector.scalar_tensor_tensor(by_group(own[:]), spread(pg[:]), row_total[:], by_group(wc[:]),
                                        ALU.mult, ALU.add)
         shared = tile("shared", [P, I], F32)
         nc.vector.scalar_tensor_tensor(by_group(shared[:]), by_group(neg_share[:]), neg_k[:], spread(group_total[:]),

from contextlib import ExitStack

import concourse.mybir as mybir

D, K, R, T, I, Q, G, U = 512, 512, 512, 2048, 512, 128, 64, 1024
FLOPS = 2 * D * Q * I + 2 * K * R * I + 2 * R * Q * I

F32 = mybir.dt.float32
BF16 = mybir.dt.bfloat16
I32 = mybir.dt.int32
U32 = mybir.dt.uint32
U16 = mybir.dt.uint16
U8 = mybir.dt.uint8
FP8X4 = mybir.dt.float8_e4m3fn_x4
FP4X4 = mybir.dt.float4_e2m1fn_x4
ALU = mybir.AluOpType
ACT = mybir.ActivationFunctionType
AX = mybir.AxisListType

P = 128
PACK = 4
GROUP = I // G
STORE_COLS = [256, 512, 512, 512, 256]
HALF = I // 2
HS_SPLIT = 320


def tile_attend_blrgated_bygroup_kernel(tc, query, keys_words, keys_scales, sharp, tab_words, tab_scales,
                                         w1, gtab, gout, hsc, old, offs2, offs, out):
    nc = tc.nc
    with ExitStack() as ctx:
        lists = ctx.enter_context(tc.tile_pool(name="lists", bufs=1))
        sb = ctx.enter_context(tc.tile_pool(name="sb", bufs=1))
        ps = ctx.enter_context(tc.psum_pool(name="ps", bufs=1))

        def tile(name, shape, dtype, tag=None):
            return sb.tile(shape, dtype, name=name, tag=tag or name, align_bytes=64)

        def by_group(ap):
            return ap.rearrange("p (g j) -> p g j", j=GROUP)

        def spread(ap):
            return ap.unsqueeze(2).to_broadcast([P, ap.shape[1], GROUP])

        def load_scale_rows(engine, plane, scales):
            for quad in range(4):
                engine.dma_start(out=plane[32 * quad:32 * quad + 4, :].bitcast(I32),
                                 in_=scales[0, 4 * quad:4 * quad + 4, :].bitcast(I32))

        slots = lists.tile([P, I // 16], U16, name="slots")
        gates = lists.tile([P, I // 16], U16, name="gates")
        key_bytes = tile("key_bytes", [P, T], U8)
        tab_bytes = tile("tab_bytes", [P, T], U8)
        scattered = tile("scattered", [P, T], F32)
        nc.vector.memset(key_bytes[:].bitcast(I32), 0)
        nc.vector.memset(tab_bytes[:].bitcast(I32), 0)
        nc.vector.memset(scattered[:], 0.0)

        q_raw = tile("q_raw", [P, PACK, Q], F32)
        key_pool = tile("key_pool", [P, T], U16)
        tab_pool = tile("tab_pool", [P, T], U16)
        w_raw = [tile("w_raw%d" % h, [P, PACK, R // 2], F32) for h in range(2)]
        g_raw = tile("g_raw", [P, PACK, Q], F32)
        gate_pool = [tile("gate_pool%d" % t, [P, U], F32) for t in range(PACK)]
        old_sb = tile("old_sb", [P, T], F32)
        sharp_sb = tile("sharp_sb", [P, 1], F32)
        hsc_sb = tile("hsc_sb", [P, PACK], F32)
        gtab_planes = gtab.rearrange("(p t) u -> t p u", t=PACK)
        w_rows = w1.rearrange("(p j) c -> p j c", j=PACK)

        nc.sync.dma_start(slots[:], offs)
        nc.sync.dma_start(out=key_pool[:].bitcast(I32), in_=keys_words[0].bitcast(I32))
        load_scale_rows(nc.sync, key_bytes, keys_scales)
        nc.sync.dma_start(out=q_raw[:], in_=query.rearrange("(p j) c -> p j c", j=PACK))
        nc.scalar.dma_start(out=sharp_sb[:], in_=sharp)
        for h in range(2):
            nc.sync.dma_start(out=w_raw[h][:], in_=w_rows[:, :, h * (R // 2):(h + 1) * (R // 2)])
        load_scale_rows(nc.sync, tab_bytes, tab_scales)
        nc.sync.dma_start(gates[:], offs2)
        nc.sync.dma_start(out=gate_pool[0][:], in_=gtab_planes[0])
        nc.sync.dma_start(out=tab_pool[:].bitcast(I32), in_=tab_words[0].bitcast(I32))
        nc.sync.dma_start(out=gate_pool[1][:], in_=gtab_planes[1])
        nc.sync.dma_start(out=hsc_sb[:], in_=hsc.rearrange("(p t) o -> p (t o)", t=PACK))
        nc.sync.dma_start(out=gate_pool[2][:], in_=gtab_planes[2])
        nc.sync.dma_start(out=gate_pool[3][:], in_=gtab_planes[3])
        nc.sync.dma_start(out=g_raw[:], in_=gout.rearrange("(p j) c -> p j c", j=PACK))
        nc.sync.dma_start(out=old_sb[:], in_=old)

        def interleaved_views(dst, src):
            return (dst.rearrange("p (c i j) -> p c j i", i=4, j=PACK), src.rearrange("p j (c i) -> p c j i", i=4))

        def quantise(name, values, width, tag=None):
            codes = tile(name + "_codes", [P, width], U32, tag)
            plane = tile(name + "_plane", [P, width], U8)
            nc.vector.quantize_mx(out=codes[:].bitcast(FP8X4), scales=plane[:], in_=values)
            return codes, plane

        halves = [slice(h * HALF, (h + 1) * HALF) for h in range(2)]
        group_halves = [slice(h * G // 2, (h + 1) * G // 2) for h in range(2)]

        key_scale = tile("key_scale", [P, I], U8)
        key_codes = tile("key_codes", [P, I], U16)
        q_bf = tile("q_bf", [P, PACK * Q], BF16)
        neg_k = tile("neg_k", [P, 1], F32)
        nc.scalar.activation(neg_k[:], sharp_sb[:], ACT.Copy, scale=-1.0 / GROUP)
        nc.vector.tensor_copy(key_codes[:], key_pool[:].indirect(slots[:]))
        nc.vector.tensor_copy(key_scale[:], key_bytes[:].indirect(slots[:]))
        dst, src = interleaved_views(q_bf[:], q_raw[:])
        nc.scalar.copy(out=dst, in_=src)
        q_codes, q_plane = quantise("q", q_bf[:], Q)
        w_bf = tile("w_bf", [P, PACK * R], BF16)
        w_dealt = w_bf[:].rearrange("p (t m j) -> p m j t", t=PACK, j=PACK)
        nc.scalar.copy(out=w_dealt[:, 0:P // 2], in_=w_raw[0][:].rearrange("p j (m t) -> p m j t", t=PACK))
        nc.vector.tensor_copy(out=w_dealt[:, P // 2:P], in_=w_raw[1][:].rearrange("p j (m t) -> p m j t", t=PACK))
        score_sum = tile("score_sum", [P, G], F32, tag="w_raw1")
        p = tile("p", [P, I], F32, tag="w_raw0")
        scores = [ps.tile([P, HALF], F32, name="score%d" % h) for h in range(2)]
        for h in range(2):
            nc.tensor.matmul_mx(out=scores[h][:], lhsT=q_codes[:].bitcast(FP8X4), lhsT_scale=q_plane[:],
                                rhs=key_codes[:, halves[h]].bitcast(FP4X4), rhs_scale=key_scale[:, halves[h]],
                                start=True, stop=True)
        for h in range(2):
            nc.vector.tensor_reduce(score_sum[:, group_halves[h]], by_group(scores[h][:]), AX.X, ALU.add)
            nc.scalar.activation(p[:, halves[h]], scores[h][:], ACT.Exp)
        neg_ms = tile("neg_ms", [P, G], F32)
        neg_top = tile("neg_top", [P, 1], F32, tag="gate")
        nc.vector.tensor_scalar(neg_ms[:], score_sum[:], neg_k[:], None, ALU.mult, ALU.min, accum_out=neg_top[:])
        pg = tile("pg", [P, G], F32)
        pg_sum = tile("pg_sum", [P, 1], F32)
        nc.scalar.activation(pg[:], neg_ms[:], ACT.Exp, bias=neg_top[:], scale=-1.0, accum_out=pg_sum[:])

        w_codes, w_plane = quantise("w", w_bf[:], R, tag="w_raw1")
        tab_scale = tile("tab_scale", [P, I], U8, tag="neg_ms")
        tab_codes = tile("tab_codes", [P, I], U16)
        nc.vector.tensor_copy(tab_scale[:], tab_bytes[:].indirect(slots[:]))
        nc.vector.tensor_copy(tab_codes[:], tab_pool[:].indirect(slots[:]))

        zh = [ps.tile([P, I], F32, name="zh%d" % t) for t in range(PACK)]
        for t in range(PACK):
            rows = slice(t * P, (t + 1) * P)
            nc.tensor.matmul_mx(out=zh[t][:], lhsT=w_codes[:, rows].bitcast(FP8X4), lhsT_scale=w_plane[:, rows],
                                rhs=tab_codes[:].bitcast(FP4X4), rhs_scale=tab_scale[:], start=True, stop=True)

        p_sum = tile("p_sum", [P, G], F32, tag="tab_pool")
        inv_s = tile("inv_s", [P, G], F32)
        inv_z = tile("inv_z", [P, 1], F32, tag="tab_bytes")
        nc.vector.tensor_reduce(p_sum[:], by_group(p[:]), AX.X, ALU.add)
        nc.vector.reciprocal(inv_z[:], pg_sum[:])
        nc.vector.reciprocal(inv_s[:], p_sum[:])

        gate = tile("gate", [P, PACK, I], F32)
        hs_planes = tile("hs_planes", [P, PACK, I], BF16)
        for t in range(PACK):
            nc.scalar.activation(gate[:, t, :], gate_pool[t][:].indirect(gates[:]), ACT.Sigmoid)
            nc.vector.scalar_tensor_tensor(hs_planes[:, t, :], zh[t][:], hsc_sb[:, t:t + 1], gate[:, t, :],
                                           ALU.mult, ALU.mult)

        g_bf = tile("g_bf", [P, PACK * Q], BF16)
        dst, src = interleaved_views(g_bf[:], g_raw[:])
        nc.scalar.copy(out=dst, in_=src)
        g_codes, g_plane = quantise("g", g_bf[:], Q)

        hs_bf = tile("hs_bf", [P, PACK * I], BF16)
        dst, src = interleaved_views(hs_bf[:, 0:PACK * HS_SPLIT], hs_planes[:, :, 0:HS_SPLIT])
        nc.vector.tensor_copy(out=dst, in_=src)
        dst, src = interleaved_views(hs_bf[:, PACK * HS_SPLIT:], hs_planes[:, :, HS_SPLIT:])
        nc.scalar.copy(out=dst, in_=src)

        neg_share = tile("neg_share", [P, I], F32, tag="gate_pool2")
        nc.vector.scalar_tensor_tensor(by_group(neg_share[:]), by_group(p[:]), -1.0, spread(inv_s[:]),
                                       ALU.mult, ALU.mult)
        weight = tile("weight", [P, I], F32)
        nc.vector.scalar_tensor_tensor(by_group(weight[:]), by_group(neg_share[:]), inv_z[:], spread(pg[:]),
                                       ALU.mult, ALU.mult)

        wc = tile("wc", [P, I], F32)
        half_total = tile("half_total", [P, 2], F32)
        c0 = []
        for h in range(2):
            hs_codes, hs_plane = quantise("hs%d" % h, hs_bf[:, PACK * h * HALF:PACK * (h + 1) * HALF], HALF)
            c0.append(ps.tile([P, HALF], F32, name="c0_%d" % h))
            nc.tensor.matmul_mx(out=c0[h][:], lhsT=g_codes[:].bitcast(FP8X4), lhsT_scale=g_plane[:],
                                rhs=hs_codes[:].bitcast(FP8X4), rhs_scale=hs_plane[:], start=True, stop=True)
        for h in range(2):
            nc.vector.scalar_tensor_tensor(wc[:, halves[h]], c0[h][:], -512.0, weight[:, halves[h]], ALU.mult, ALU.mult,
                                           accum_out=half_total[:, h:h + 1])
        row_factor = tile("row_factor", [P, 1], F32, tag="gate_pool3")
        first_term = tile("first_term", [P, 1], F32)
        row_total = tile("row_total", [P, 1], F32)
        nc.scalar.activation(row_factor[:], inv_z[:], ACT.Copy, scale=neg_k[:])
        nc.scalar.activation(first_term[:], half_total[:, 0:1], ACT.Copy, scale=row_factor[:])
        nc.scalar.activation(row_total[:], half_total[:, 1:2], ACT.Identity, bias=first_term[:], scale=row_factor[:])
        group_total = tile("group_total", [P, G], F32)
        for h in range(2):
            nc.vector.tensor_reduce(group_total[:, group_halves[h]], by_group(wc[:, halves[h]]), AX.X, ALU.add)
        own = tile("own", [P, I], F32)
        nc.vector.scalar_tensor_tensor(by_group(own[:]), spread(pg[:]), row_total[:], by_group(wc[:]),
                                       ALU.mult, ALU.add)
        shared = tile("shared", [P, I], F32)
        nc.vector.scalar_tensor_tensor(by_group(shared[:]), by_group(neg_share[:]), neg_k[:], spread(group_total[:]),
                                       ALU.subtract, ALU.mult)
        nc.vector.tensor_tensor(scattered[:].indirect(slots[:]), own[:], shared[:], ALU.add)

        first = 0
        for n, width in enumerate(STORE_COLS):
            cols = slice(first, first + width)
            result = tile("result%d" % n, [P, width], F32)
            nc.vector.tensor_tensor(result[:], scattered[:, cols], old_sb[:, cols], ALU.add)
            nc.sync.dma_start(out=out[:, cols], in_=result[:])
            first += width
